import numpy as np
import ml_dtypes


def mxq(x, axis, fmt="e4m3"):
    dtype, down = {"e4m3": (ml_dtypes.float8_e4m3fn, 7), "e5m2": (ml_dtypes.float8_e5m2, 14)}[fmt]
    v = np.moveaxis(np.asarray(x, np.float32).astype(ml_dtypes.bfloat16).astype(np.float64), axis, -1)
    blocks = v.reshape(v.shape[:-1] + (-1, 32))
    amax = np.abs(blocks).max(-1, keepdims=True)
    byte = np.maximum(np.where(amax > 0, np.frexp(amax)[1] - 1 + 127, 0) - down, 1)
    scale = np.exp2(byte - 127.0)
    codes = (blocks / scale).astype(np.float32).astype(dtype).astype(np.float64)
    return np.moveaxis((codes * scale).reshape(v.shape), -1, axis)


WIDE = False


def mx_kscale(k):
    if not WIDE:
        return np.ones(k)
    levels = np.array([10, -10, 5, -5, 0])
    if k % 512:
        return np.exp2(np.random.permutation(np.resize(levels, k // 32))).repeat(32)
    a = np.empty((k // 512, 16))
    for p in range(k // 512):
        a[p, :8] = np.random.permutation(np.resize(levels, 8))
        for g in range(8):
            far = levels[np.abs(levels - a[p, g]) >= 10]
            a[p, g + 8] = far[np.random.randint(len(far))]
    return np.exp2(a.ravel()).repeat(32)


def f64(x):
    return np.asarray(x).astype(np.float64)


def striped(idx):
    return np.tile(idx.reshape(-1, 16).T, (8, 1)).astype(np.uint16)


def unstriped(offs):
    return offs[:16].T.reshape(-1).astype(np.int64)


def pack_weight(w):
    k, n = w.shape
    w = f64(np.asarray(w, np.float32).astype(ml_dtypes.bfloat16)).reshape(k // 32, 32, n)
    amax = np.abs(w).max(1)
    byte = np.clip(np.where(amax > 0, np.frexp(amax)[1] - 1 + 127 - 7, 1), 1, 254)
    scaled = (w * np.exp2(127.0 - byte)[:, None, :]).reshape(k, n).astype(np.float32)
    words = np.ascontiguousarray(scaled.reshape(k // 512, 128, 4, n).transpose(0, 1, 3, 2)).astype(ml_dtypes.float8_e4m3fn).view(np.uint8)
    return words, np.ascontiguousarray(byte.astype(np.uint8).reshape(k // 512, 16, n))


def unpack_weight(words, scales):
    g, p, n, _ = words.shape
    vals = np.ascontiguousarray(words).view(ml_dtypes.float8_e4m3fn).astype(np.float64) * np.repeat(np.exp2(scales.astype(np.float64) - 127.0), 8, axis=1)[..., None]
    return vals.transpose(0, 1, 3, 2).reshape(g * 512, n)


def silu(v):
    return v / (1.0 + np.exp(-np.maximum(v, -700.0)))


K, T, E, C, N = 1024, 1024, 8, 128, 128


def by_expert(wq, xq):
    return np.concatenate([wq[e].T @ xq[:, e * C:(e + 1) * C] for e in range(E)], axis=1)


def setup_inputs():
    n = np.random.standard_normal
    s = mx_kscale(K)[:, None]
    packed = [pack_weight(m) for m in n((E, K, N)) / np.sqrt(K) / s[None]]
    return {
        "xT": (n((K, T)) * s).astype(np.float32),
        "w_words": np.stack([m[0] for m in packed]),
        "w_scales": np.stack([m[1] for m in packed]),
        "b": (0.3 * n((N, E))).astype(np.float32),
        "gate": np.tile(np.random.uniform(0.2, 1.0, E * C), (N, 1)).astype(np.float32),
        "offs": striped(np.random.permutation(T)[:E * C]),
    }


def reference(xT, w_words, w_scales, b, gate, offs):
    idx = unstriped(offs)
    xq = mxq(f64(xT)[:, idx], 0, "e4m3")
    w = np.stack([unpack_weight(w_words[e], w_scales[e]) for e in range(E)])
    y = by_expert(w, xq)
    y = silu(y + np.repeat(f64(b), C, axis=1))
    out = np.zeros((N, T))
    out[:, idx] = f64(gate) * y
    return out

@@ -1,0 +1,140 @@
+from contextlib import ExitStack
+
+import concourse.mybir as mybir
+
+K, T, E, C, N = 1024, 1024, 8, 128, 128
+P = 128
+PASSES = 2
+W = 1408
+FLOPS = 2 * K * E * C * N
+
+F32 = mybir.dt.float32
+BF16 = mybir.dt.bfloat16
+I32 = mybir.dt.int32
+U32 = mybir.dt.uint32
+U16 = mybir.dt.uint16
+U8 = mybir.dt.uint8
+FP8X4 = mybir.dt.float8_e4m3fn_x4
+ACT = mybir.ActivationFunctionType
+MULT = mybir.AluOpType.mult
+
+
+def tile_routed_moe_kernel(tc, xT, w_words, w_scales, b, gate, offs, out):
+    nc = tc.nc
+    x_view = xT.rearrange("(a p j) t -> a p j t", p=P, j=4)
+
+    with ExitStack() as ctx:
+        keep = ctx.enter_context(tc.tile_pool(name="keep", bufs=1))
+        psum = ctx.enter_context(tc.psum_pool(name="psum", bufs=1))
+
+        offsets = keep.tile([P, E * C // 16], U16, name="offsets")
+        scale_bytes = keep.tile([P, W], U8, name="scale_bytes", align_bytes=64)
+        w_scale = keep.tile([P, E * PASSES, N], U8, name="w_scale", align_bytes=64)
+        w_code = keep.tile([P, E * PASSES, N], U32, name="w_code", align_bytes=64)
+        gates = keep.tile([P, E * C], F32, name="gates")
+        bias = keep.tile([P, E], F32, name="bias")
+        warm = keep.tile([P, 1], F32, name="warm")
+        result = keep.tile([P, T], F32, name="result")
+
+        chunks = [(0, 0, 512), (0, 512, 512), (1, 0, 512), (1, 512, 256), (1, 768, 256)]
+        raws = []
+        for a, t0, w in chunks:
+            raw = keep.tile([P, 4, w], F32, name=f"raw_{a}_{t0}")
+            nc.sync.dma_start(out=raw[:], in_=x_view[a, :, :, t0 : t0 + w])
+            raws.append(raw)
+            if len(raws) == 1:
+                nc.sync.dma_start(offsets[:], offs)
+        nc.gpsimd.memset(scale_bytes[:], 0)
+        nc.vector.memset(w_scale[:].rearrange("p g n -> p (g n)").bitcast(I32), 0)
+        nc.scalar.dma_start(out=bias[:], in_=b)
+        ws_view = w_scales.rearrange("e a q n -> q (e a) n")
+        for q in range(4):
+            nc.sync.dma_start(out=w_scale[32 * q : 32 * q + 4, :, :].bitcast(I32), in_=ws_view[4 * q : 4 * q + 4, :, :].bitcast(I32))
+        ww_view = w_words.rearrange("e a p n r -> p (e a) (n r)").bitcast(I32)
+        for h in range(2):
+            nc.sync.dma_start(out=w_code[:, 8 * h : 8 * h + 8, :].bitcast(I32), in_=ww_view[:, 8 * h : 8 * h + 8, :])
+        nc.sync.dma_start(out=gates[:], in_=gate)
+
+        nc.vector.memset(warm[:], 0.0)
+        nc.scalar.activation(warm[:], warm[:], ACT.Silu)
+
+        words = [keep.tile([P, T], U32, name=f"words_{a}", align_bytes=64) for a in range(PASSES)]
+        mixed = {}
+
+        def cast(engine, i, u, n):
+            a, t0, w = chunks[i]
+            m = keep.tile([P, n, 4], BF16, name=f"mixed_{a}_{t0 + u}", align_bytes=64)
+            src = raws[i][:, :, u : u + n].rearrange("p j t -> p t j")
+            if engine == "s":
+                nc.scalar.copy(out=m[:], in_=src)
+            else:
+                nc.vector.tensor_copy(out=m[:], in_=src)
+            mixed[(a, t0 + u)] = (m, n)
+
+        def quantise(a, t):
+            m, n = mixed[(a, t)]
+            nc.vector.quantize_mx(
+                out=words[a][:, t : t + n].bitcast(FP8X4),
+                scales=scale_bytes[4 * a : P, t : t + n],
+                in_=m[:].rearrange("p t j -> p (t j)"),
+            )
+
+        def gather_words(a, s, n):
+            g = keep.tile([P, n], U32, name=f"gathered_{a}_{s}", align_bytes=64)
+            nc.vector.tensor_copy(g[:], words[a][:].indirect(offsets[:, s // 16 : (s + n) // 16]))
+            return g
+
+        cast("s", 0, 0, 256)
+        cast("v", 0, 256, 256)
+        cast("s", 1, 0, 256)
+        quantise(0, 256)
+        quantise(0, 0)
+        cast("v", 1, 256, 256)
+        quantise(0, 768)
+        quantise(0, 512)
+        cast("s", 2, 0, 256)
+        cast("s", 2, 256, 256)
+        g0 = [gather_words(0, s, 512) for s in (0, 512)]
+        quantise(1, 0)
+        quantise(1, 256)
+        cast("v", 3, 0, 256)
+        cast("s", 4, 0, 128)
+        cast("v", 4, 128, 128)
+        quantise(1, 512)
+        quantise(1, 896)
+        quantise(1, 768)
+
+        slot_bytes = keep.tile([P, E * C], U8, name="slot_bytes", align_bytes=64)
+        nc.vector.tensor_copy(slot_bytes[:], scale_bytes[:].indirect(offsets[:]))
+        acc = [psum.tile([P, C], F32, name=f"acc_{e}") for e in range(E)]
+
+        def multiply(e, a, g, col):
+            nc.tensor.matmul_mx(
+                out=acc[e][:],
+                lhsT=w_code[:, PASSES * e + a, :].bitcast(FP8X4),
+                lhsT_scale=w_scale[:, PASSES * e + a, :],
+                rhs=g[:, col : col + C].bitcast(FP8X4),
+                rhs_scale=slot_bytes[4 * a : P, C * e : C * e + C],
+                start=(a == 0),
+                stop=(a == PASSES - 1),
+            )
+
+        for e in range(E):
+            multiply(e, 0, g0[e // 4], C * (e % 4))
+
+        pieces = [(0, 256), (256, 256), (512, 512)]
+        values = []
+        for s, n in pieces:
+            g = gather_words(1, s, n)
+            y = keep.tile([P, n], F32, name=f"y_{s}")
+            z = keep.tile([P, n], F32, name=f"z_{s}")
+            for col in range(0, n, C):
+                e = (s + col) // C
+                multiply(e, 1, g, col)
+                nc.scalar.activation(y[:, col : col + C], acc[e][:], ACT.Silu, bias=bias[:, e : e + 1])
+            for col in range(0, n, 256):
+                nc.gpsimd.tensor_tensor(z[:, col : col + 256], y[:, col : col + 256], gates[:, s + col : s + col + 256], MULT)
+            values.append(z)
+        for (s, n), z in zip(pieces, values):
+            nc.vector.tensor_copy(result[:].indirect(offsets[:, s // 16 : (s + n) // 16]), z[:])
+        nc.sync.dma_start(out=out, in_=result[:])

@@ -64,11 +64,16 @@ def tile_routed_moe_kernel(tc, xT, w_words, w_scales, b, gate, offs, out):
         def cast(engine, i, u, n):
             a, t0, w = chunks[i]
             m = keep.tile([P, n, 4], BF16, name=f"mixed_{a}_{t0 + u}", align_bytes=64)
-            src = raws[i][:, :, u : u + n].rearrange("p j t -> p t j")
-            if engine == "s":
-                nc.scalar.copy(out=m[:], in_=src)
+            src = raws[i][:, :, u : u + n]
+            if engine == "g":
+                nc.gpsimd.tensor_copy(out=m[:], in_=src.rearrange("p j t -> p t j"))
             else:
-                nc.vector.tensor_copy(out=m[:], in_=src)
+                dst = m[:].rearrange("p (c i) j -> p c j i", i=4)
+                src = src.rearrange("p j (c i) -> p c j i", i=4)
+                if engine == "s":
+                    nc.scalar.copy(out=dst, in_=src)
+                else:
+                    nc.vector.tensor_copy(out=dst, in_=src)
             mixed[(a, t0 + u)] = (m, n)
 
         def quantise(a, t):
@@ -92,16 +97,16 @@ def tile_routed_moe_kernel(tc, xT, w_words, w_scales, b, gate, offs, out):
         cast("v", 1, 256, 256)
         quantise(0, 768)
         quantise(0, 512)
-        cast("s", 2, 0, 256)
+        cast("g", 2, 0, 128)
+        cast("s", 2, 128, 128)
         cast("s", 2, 256, 256)
         g0 = [gather_words(0, s, 512) for s in (0, 512)]
-        quantise(1, 0)
+        quantise(1, 128)
         quantise(1, 256)
-        cast("v", 3, 0, 256)
-        cast("s", 4, 0, 128)
-        cast("v", 4, 128, 128)
+        quantise(1, 0)
+        cast("s", 3, 0, 256)
+        cast("v", 4, 0, 256)
         quantise(1, 512)
-        quantise(1, 896)
         quantise(1, 768)
 
         slot_bytes = keep.tile([P, E * C], U8, name="slot_bytes", align_bytes=64)
@@ -122,19 +127,15 @@ def tile_routed_moe_kernel(tc, xT, w_words, w_scales, b, gate, offs, out):
         for e in range(E):
             multiply(e, 0, g0[e // 4], C * (e % 4))
 
-        pieces = [(0, 256), (256, 256), (512, 512)]
-        values = []
-        for s, n in pieces:
+        y = keep.tile([P, E * C], F32, name="y")
+        for s, n in ((0, 256), (256, 768)):
             g = gather_words(1, s, n)
-            y = keep.tile([P, n], F32, name=f"y_{s}")
-            z = keep.tile([P, n], F32, name=f"z_{s}")
             for col in range(0, n, C):
                 e = (s + col) // C
                 multiply(e, 1, g, col)
-                nc.scalar.activation(y[:, col : col + C], acc[e][:], ACT.Silu, bias=bias[:, e : e + 1])
-            for col in range(0, n, 256):
-                nc.gpsimd.tensor_tensor(z[:, col : col + 256], y[:, col : col + 256], gates[:, s + col : s + col + 256], MULT)
-            values.append(z)
-        for (s, n), z in zip(pieces, values):
-            nc.vector.tensor_copy(result[:].indirect(offsets[:, s // 16 : (s + n) // 16]), z[:])
+                nc.scalar.activation(y[:, C * e : C * e + C], acc[e][:], ACT.Silu, bias=bias[:, e : e + 1])
+        for s, n in ((0, 256), (256, 256), (512, 512)):
+            nc.vector.tensor_tensor(
+                result[:].indirect(offsets[:, s // 16 : (s + n) // 16]), y[:, s : s + n], gates[:, s : s + n], MULT
+            )
         nc.sync.dma_start(out=out, in_=result[:])

@@ -34,7 +34,7 @@ def tile_routed_moe_kernel(tc, xT, w_words, w_scales, b, gate, offs, out):
         gates = keep.tile([P, E * C], F32, name="gates")
         bias = keep.tile([P, E], F32, name="bias")
         warm = keep.tile([P, 1], F32, name="warm")
-        result = keep.tile([P, T], F32, name="result")
+        result = keep.tile([P, W], F32, name="result")
 
         chunks = [(0, 0, 512), (0, 512, 512), (1, 0, 512), (1, 512, 256), (1, 768, 256)]
         raws = []
@@ -46,42 +46,44 @@ def tile_routed_moe_kernel(tc, xT, w_words, w_scales, b, gate, offs, out):
                 nc.sync.dma_start(offsets[:], offs)
         nc.gpsimd.memset(scale_bytes[:], 0)
         nc.vector.memset(w_scale[:].rearrange("p g n -> p (g n)").bitcast(I32), 0)
-        nc.scalar.dma_start(out=bias[:], in_=b)
         ws_view = w_scales.rearrange("e a q n -> q (e a) n")
         for q in range(4):
             nc.sync.dma_start(out=w_scale[32 * q : 32 * q + 4, :, :].bitcast(I32), in_=ws_view[4 * q : 4 * q + 4, :, :].bitcast(I32))
         ww_view = w_words.rearrange("e a p n r -> p (e a) (n r)").bitcast(I32)
-        for h in range(2):
-            nc.sync.dma_start(out=w_code[:, 8 * h : 8 * h + 8, :].bitcast(I32), in_=ww_view[:, 8 * h : 8 * h + 8, :])
+        nc.sync.dma_start(out=bias[:], in_=b)
+        nc.sync.dma_start(out=w_code[:, 0:8, :].bitcast(I32), in_=ww_view[:, 0:8, :])
         nc.sync.dma_start(out=gates[:], in_=gate)
+        nc.sync.dma_start(out=w_code[:, 8:16, :].bitcast(I32), in_=ww_view[:, 8:16, :])
 
         nc.vector.memset(warm[:], 0.0)
         nc.scalar.activation(warm[:], warm[:], ACT.Silu)
 
-        words = [keep.tile([P, T], U32, name=f"words_{a}", align_bytes=64) for a in range(PASSES)]
+        words = [keep.tile([P, W], U32, name=f"words_{a}", align_bytes=64) for a in range(PASSES)]
         mixed = {}
 
         def cast(engine, i, u, n):
             a, t0, w = chunks[i]
-            m = keep.tile([P, n, 4], BF16, name=f"mixed_{a}_{t0 + u}", align_bytes=64)
+            if i not in mixed:
+                m = keep.tile([P, w, 4], BF16, name=f"mixed_{a}_{t0}", align_bytes=64)
+                mixed[i] = m
+            part = mixed[i][:, u : u + n, :]
             src = raws[i][:, :, u : u + n]
             if engine == "g":
-                nc.gpsimd.tensor_copy(out=m[:], in_=src.rearrange("p j t -> p t j"))
+                nc.gpsimd.tensor_copy(out=part, in_=src.rearrange("p j t -> p t j"))
             else:
-                dst = m[:].rearrange("p (c i) j -> p c j i", i=4)
+                dst = part.rearrange("p (c i) j -> p c j i", i=4)
                 src = src.rearrange("p j (c i) -> p c j i", i=4)
                 if engine == "s":
                     nc.scalar.copy(out=dst, in_=src)
                 else:
                     nc.vector.tensor_copy(out=dst, in_=src)
-            mixed[(a, t0 + u)] = (m, n)
 
-        def quantise(a, t):
-            m, n = mixed[(a, t)]
+        def quantise(i, u, n):
+            a, t0, w = chunks[i]
             nc.vector.quantize_mx(
-                out=words[a][:, t : t + n].bitcast(FP8X4),
-                scales=scale_bytes[4 * a : P, t : t + n],
-                in_=m[:].rearrange("p t j -> p (t j)"),
+                out=words[a][:, t0 + u : t0 + u + n].bitcast(FP8X4),
+                scales=scale_bytes[4 * a : P, t0 + u : t0 + u + n],
+                in_=mixed[i][:, u : u + n, :].rearrange("p t j -> p (t j)"),
             )
 
         def gather_words(a, s, n):
@@ -89,25 +91,20 @@ def tile_routed_moe_kernel(tc, xT, w_words, w_scales, b, gate, offs, out):
             nc.vector.tensor_copy(g[:], words[a][:].indirect(offsets[:, s // 16 : (s + n) // 16]))
             return g
 
-        cast("s", 0, 0, 256)
-        cast("v", 0, 256, 256)
-        cast("s", 1, 0, 256)
-        quantise(0, 256)
-        quantise(0, 0)
-        cast("v", 1, 256, 256)
-        quantise(0, 768)
-        quantise(0, 512)
+        cast("s", 0, 0, 192)
+        cast("v", 0, 192, 320)
+        quantise(0, 0, 512)
+        cast("s", 1, 0, 192)
+        cast("v", 1, 192, 320)
+        quantise(1, 0, 512)
         cast("g", 2, 0, 128)
-        cast("s", 2, 128, 128)
-        cast("s", 2, 256, 256)
-        g0 = [gather_words(0, s, 512) for s in (0, 512)]
-        quantise(1, 128)
-        quantise(1, 256)
-        quantise(1, 0)
+        cast("s", 2, 128, 384)
+        g0 = gather_words(0, 0, 1024)
+        quantise(2, 0, 512)
         cast("s", 3, 0, 256)
         cast("v", 4, 0, 256)
-        quantise(1, 512)
-        quantise(1, 768)
+        quantise(3, 0, 256)
+        quantise(4, 0, 256)
 
         slot_bytes = keep.tile([P, E * C], U8, name="slot_bytes", align_bytes=64)
         nc.vector.tensor_copy(slot_bytes[:], scale_bytes[:].indirect(offsets[:]))
@@ -125,17 +122,17 @@ def tile_routed_moe_kernel(tc, xT, w_words, w_scales, b, gate, offs, out):
             )
 
         for e in range(E):
-            multiply(e, 0, g0[e // 4], C * (e % 4))
+            multiply(e, 0, g0, C * e)
 
         y = keep.tile([P, E * C], F32, name="y")
-        for s, n in ((0, 256), (256, 768)):
+        for s, n in ((0, 384), (384, 640)):
             g = gather_words(1, s, n)
             for col in range(0, n, C):
                 e = (s + col) // C
                 multiply(e, 1, g, col)
                 nc.scalar.activation(y[:, C * e : C * e + C], acc[e][:], ACT.Silu, bias=bias[:, e : e + 1])
-        for s, n in ((0, 256), (256, 256), (512, 512)):
+        for s, n in ((0, 384), (384, 640)):
             nc.vector.tensor_tensor(
                 result[:].indirect(offsets[:, s // 16 : (s + n) // 16]), y[:, s : s + n], gates[:, s : s + n], MULT
             )
-        nc.sync.dma_start(out=out, in_=result[:])
+        nc.sync.dma_start(out=out, in_=result[:, 0:T])

from contextlib import ExitStack

import concourse.mybir as mybir

K, T, E, C, N = 1024, 1024, 8, 128, 128
P = 128
PASSES = 2
W = 1408
FLOPS = 2 * K * E * C * N

F32 = mybir.dt.float32
BF16 = mybir.dt.bfloat16
I32 = mybir.dt.int32
U32 = mybir.dt.uint32
U16 = mybir.dt.uint16
U8 = mybir.dt.uint8
FP8X4 = mybir.dt.float8_e4m3fn_x4
ACT = mybir.ActivationFunctionType
MULT = mybir.AluOpType.mult


def tile_routed_moe_kernel(tc, xT, w_words, w_scales, b, gate, offs, out):
    nc = tc.nc
    x_view = xT.rearrange("(a p j) t -> a p j t", p=P, j=4)

    with ExitStack() as ctx:
        keep = ctx.enter_context(tc.tile_pool(name="keep", bufs=1))
        psum = ctx.enter_context(tc.psum_pool(name="psum", bufs=1))

        offsets = keep.tile([P, E * C // 16], U16, name="offsets")
        scale_bytes = keep.tile([P, W], U8, name="scale_bytes", align_bytes=64)
        w_scale = keep.tile([P, E * PASSES, N], U8, name="w_scale", align_bytes=64)
        w_code = keep.tile([P, E * PASSES, N], U32, name="w_code", align_bytes=64)
        gates = keep.tile([P, E * C], F32, name="gates")
        bias = keep.tile([P, E], F32, name="bias")
        warm = keep.tile([P, 1], F32, name="warm")
        result = keep.tile([P, W], F32, name="result")

        chunks = [(0, 0, 512), (0, 512, 512), (1, 0, 512), (1, 512, 256), (1, 768, 256)]
        raws = []
        for a, t0, w in chunks:
            raw = keep.tile([P, 4, w], F32, name=f"raw_{a}_{t0}")
            nc.sync.dma_start(out=raw[:], in_=x_view[a, :, :, t0 : t0 + w])
            raws.append(raw)
            if len(raws) == 1:
                nc.sync.dma_start(offsets[:], offs)
        nc.gpsimd.memset(scale_bytes[:], 0)
        nc.vector.memset(w_scale[:].rearrange("p g n -> p (g n)").bitcast(I32), 0)
        ws_view = w_scales.rearrange("e a q n -> q (e a) n")
        for q in range(4):
            nc.sync.dma_start(out=w_scale[32 * q : 32 * q + 4, :, :].bitcast(I32), in_=ws_view[4 * q : 4 * q + 4, :, :].bitcast(I32))
        ww_view = w_words.rearrange("e a p n r -> p (e a) (n r)").bitcast(I32)
        nc.sync.dma_start(out=bias[:], in_=b)
        nc.sync.dma_start(out=w_code[:, 0:8, :].bitcast(I32), in_=ww_view[:, 0:8, :])
        nc.sync.dma_start(out=gates[:], in_=gate)
        nc.sync.dma_start(out=w_code[:, 8:16, :].bitcast(I32), in_=ww_view[:, 8:16, :])

        nc.vector.memset(warm[:], 0.0)
        nc.scalar.activation(warm[:], warm[:], ACT.Silu)

        words = [keep.tile([P, W], U32, name=f"words_{a}", align_bytes=64) for a in range(PASSES)]
        mixed = {}

        def cast(engine, i, u, n):
            a, t0, w = chunks[i]
            if i not in mixed:
                m = keep.tile([P, w, 4], BF16, name=f"mixed_{a}_{t0}", align_bytes=64)
                mixed[i] = m
            part = mixed[i][:, u : u + n, :]
            src = raws[i][:, :, u : u + n]
            if engine == "g":
                nc.gpsimd.tensor_copy(out=part, in_=src.rearrange("p j t -> p t j"))
            else:
                dst = part.rearrange("p (c i) j -> p c j i", i=4)
                src = src.rearrange("p j (c i) -> p c j i", i=4)
                if engine == "s":
                    nc.scalar.copy(out=dst, in_=src)
                else:
                    nc.vector.tensor_copy(out=dst, in_=src)

        def quantise(i, u, n):
            a, t0, w = chunks[i]
            nc.vector.quantize_mx(
                out=words[a][:, t0 + u : t0 + u + n].bitcast(FP8X4),
                scales=scale_bytes[4 * a : P, t0 + u : t0 + u + n],
                in_=mixed[i][:, u : u + n, :].rearrange("p t j -> p (t j)"),
            )

        def gather_words(a, s, n):
            g = keep.tile([P, n], U32, name=f"gathered_{a}_{s}", align_bytes=64)
            nc.vector.tensor_copy(g[:], words[a][:].indirect(offsets[:, s // 16 : (s + n) // 16]))
            return g

        cast("s", 0, 0, 192)
        cast("v", 0, 192, 320)
        quantise(0, 0, 512)
        cast("s", 1, 0, 192)
        cast("v", 1, 192, 320)
        quantise(1, 0, 512)
        cast("g", 2, 0, 128)
        cast("s", 2, 128, 384)
        g0 = gather_words(0, 0, 1024)
        quantise(2, 0, 512)
        cast("s", 3, 0, 256)
        cast("v", 4, 0, 256)
        quantise(3, 0, 256)
        quantise(4, 0, 256)

        slot_bytes = keep.tile([P, E * C], U8, name="slot_bytes", align_bytes=64)
        nc.vector.tensor_copy(slot_bytes[:], scale_bytes[:].indirect(offsets[:]))
        acc = [psum.tile([P, C], F32, name=f"acc_{e}") for e in range(E)]

        def multiply(e, a, g, col):
            nc.tensor.matmul_mx(
                out=acc[e][:],
                lhsT=w_code[:, PASSES * e + a, :].bitcast(FP8X4),
                lhsT_scale=w_scale[:, PASSES * e + a, :],
                rhs=g[:, col : col + C].bitcast(FP8X4),
                rhs_scale=slot_bytes[4 * a : P, C * e : C * e + C],
                start=(a == 0),
                stop=(a == PASSES - 1),
            )

        for e in range(E):
            multiply(e, 0, g0, C * e)

        y = keep.tile([P, E * C], F32, name="y")
        for s, n in ((0, 384), (384, 640)):
            g = gather_words(1, s, n)
            for col in range(0, n, C):
                e = (s + col) // C
                multiply(e, 1, g, col)
                nc.scalar.activation(y[:, C * e : C * e + C], acc[e][:], ACT.Silu, bias=bias[:, e : e + 1])
        for s, n in ((0, 384), (384, 640)):
            nc.vector.tensor_tensor(
                result[:].indirect(offsets[:, s // 16 : (s + n) // 16]), y[:, s : s + n], gates[:, s : s + n], MULT
            )
        nc.sync.dma_start(out=out, in_=result[:, 0:T])
